import numpy as np
import ml_dtypes


def mxq(x, axis, fmt="e4m3"):
    dtype, down = {"e4m3": (ml_dtypes.float8_e4m3fn, 7), "e5m2": (ml_dtypes.float8_e5m2, 14)}[fmt]
    v = np.moveaxis(np.asarray(x, np.float32).astype(ml_dtypes.bfloat16).astype(np.float64), axis, -1)
    blocks = v.reshape(v.shape[:-1] + (-1, 32))
    amax = np.abs(blocks).max(-1, keepdims=True)
    byte = np.maximum(np.where(amax > 0, np.frexp(amax)[1] - 1 + 127, 0) - down, 1)
    scale = np.exp2(byte - 127.0)
    codes = (blocks / scale).astype(np.float32).astype(dtype).astype(np.float64)
    return np.moveaxis((codes * scale).reshape(v.shape), -1, axis)


WIDE = False


def mx_kscale(k):
    if not WIDE:
        return np.ones(k)
    levels = np.array([10, -10, 5, -5, 0])
    if k % 512:
        return np.exp2(np.random.permutation(np.resize(levels, k // 32))).repeat(32)
    a = np.empty((k // 512, 16))
    for p in range(k // 512):
        a[p, :8] = np.random.permutation(np.resize(levels, 8))
        for g in range(8):
            far = levels[np.abs(levels - a[p, g]) >= 10]
            a[p, g + 8] = far[np.random.randint(len(far))]
    return np.exp2(a.ravel()).repeat(32)


def f64(x):
    return np.asarray(x).astype(np.float64)


def striped(idx):
    return np.tile(np.asarray(idx).reshape(-1, 16).T, (8, 1)).astype(np.uint16)


def unstriped(offs):
    return offs[:16].T.reshape(-1).astype(np.int64)


E2M1 = np.array([0.0, 0.5, 1.0, 1.5, 2.0, 3.0, 4.0, 6.0, -0.0, -0.5, -1.0, -1.5, -2.0, -3.0, -4.0, -6.0])


def pack_weight(w, fmt):
    k, n = w.shape
    w = f64(np.asarray(w, np.float32).astype(ml_dtypes.bfloat16)).reshape(k // 32, 32, n)
    amax = np.abs(w).max(1)
    if fmt == "e4m3":
        byte = np.frexp(amax)[1] - 1 + 127 - 7
    else:
        mant, ex = np.frexp(amax / 6.0)
        byte = np.where(mant > 0.5, ex, ex - 1) + 127
    byte = np.clip(np.where(amax > 0, byte, 1), 1, 254)
    scaled = (w * np.exp2(127.0 - byte)[:, None, :]).reshape(k, n).astype(np.float32)
    by_word = np.ascontiguousarray(scaled.reshape(k // 512, 128, 4, n).transpose(0, 1, 3, 2))
    if fmt == "e4m3":
        words = by_word.astype(ml_dtypes.float8_e4m3fn).view(np.uint8)
    else:
        c = by_word.astype(ml_dtypes.float4_e2m1fn).view(np.uint8) & 0xF
        words = (c[..., 0::2] | (c[..., 1::2] << 4)).reshape(k // 512, 128, 2 * n)
    return np.ascontiguousarray(words), np.ascontiguousarray(byte.astype(np.uint8).reshape(k // 512, 16, n))


def unpack_weight(words, scales, fmt):
    g, _, n = scales.shape
    words = np.ascontiguousarray(words).reshape(g, 128, n, -1)
    if fmt == "e4m3":
        vals = words.view(ml_dtypes.float8_e4m3fn).astype(np.float64)
    else:
        nib = np.empty((g, 128, n, 4), np.uint8)
        nib[..., 0::2] = words & 0xF
        nib[..., 1::2] = words >> 4
        vals = E2M1[nib]
    vals = vals * np.repeat(np.exp2(scales.astype(np.float64) - 127.0), 8, axis=1)[..., None]
    return vals.transpose(0, 1, 3, 2).reshape(g * 512, n)


D, T, I, Q, E = 512, 2048, 512, 128, 512


def setup_inputs():
    n = np.random.standard_normal
    idx = np.random.permutation(T)[:I]
    fd = mx_kscale(D)
    fi = mx_kscale(I)
    ti = np.ones(T)
    ti[idx] = fi
    keysp = pack_weight(n((D, T)) / fd[:, None], "e2m1")
    return {
        "query": (n((D, Q)) * 0.25 / np.sqrt(D) * fd[:, None]).astype(np.float32),
        "keys_words": keysp[0],
        "keys_scales": keysp[1],
        "m0": (np.random.uniform(0.3, 1.2, (Q, 1))).astype(np.float32),
        "z0": (np.random.uniform(100.0, 500.0, (Q, 1))).astype(np.float32),
        "o0": (n((Q, E)) * 0.06).astype(np.float32),
        "size": (np.random.uniform(0.5, 2.0, (1, I)) * fi).astype(np.float32),
        "vals": (n((E, T)) / ti).astype(np.float32),
        "offs": striped(idx),
    }


def reference(query, keys_words, keys_scales, m0, z0, o0, size, vals, offs):
    idx = unstriped(offs)
    keysu = unpack_weight(keys_words, keys_scales, "e2m1")
    queryq = mxq(f64(query), 0, "e4m3")
    keysidxg = keysu[:, idx]
    a = queryq.T @ keysidxg
    m1 = np.maximum(np.max(a, axis=1, keepdims=True), f64(m0))
    p = np.exp(a - m1)
    r0 = f64(z0) * np.exp(f64(m0) - m1)
    z = np.sum(p, axis=1, keepdims=True) + r0
    w = p * f64(size)
    wt = w.T
    vt = f64(vals)[:, idx].T
    wtq = mxq(wt, 0, "e4m3")
    vtq = mxq(vt, 0, "e4m3")
    o = wtq.T @ vtq
    y = (o + f64(o0) * r0) / z
    return y

@@ -1,0 +1,159 @@
+from contextlib import ExitStack
+
+import concourse.mybir as mybir
+from concourse.masks import make_identity
+
+D, T, I, Q, E = 512, 2048, 512, 128, 512
+FLOPS = 2 * Q * I * D + 2 * Q * I * E
+
+F32 = mybir.dt.float32
+BF16 = mybir.dt.bfloat16
+I32 = mybir.dt.int32
+U32 = mybir.dt.uint32
+U16 = mybir.dt.uint16
+U8 = mybir.dt.uint8
+FP8X4 = mybir.dt.float8_e4m3fn_x4
+FP4X4 = mybir.dt.float4_e2m1fn_x4
+ALU = mybir.AluOpType
+ACT = mybir.ActivationFunctionType
+
+P = 128
+PACK = 4
+BLOCKS = E // P
+
+
+def tile_attend_resumedread_kernel(tc, query, keys_words, keys_scales, m0, z0, o0, size, vals, offs, out):
+    nc = tc.nc
+    with ExitStack() as ctx:
+        sb = ctx.enter_context(tc.tile_pool(name="sb", bufs=1))
+        ps = ctx.enter_context(tc.psum_pool(name="ps", bufs=1))
+
+        offsets = sb.tile([P, I // 16], U16, name="offsets")
+        key_words = sb.tile([P, T], U16, name="key_words", align_bytes=64)
+        key_bytes = sb.tile([P, T], U8, name="key_bytes", align_bytes=64)
+        q_raw = sb.tile([P, PACK, Q], F32, name="q_raw")
+        v_pool = [sb.tile([P, T], F32, name="v_pool%d" % b) for b in range(BLOCKS)]
+        m0_sb = sb.tile([P, 1], F32, name="m0_sb")
+        z0_sb = sb.tile([P, 1], F32, name="z0_sb")
+        size_sb = sb.tile([P, PACK], F32, name="size_sb")
+        o0_sb = sb.tile([P, E], F32, name="o0_sb")
+        ident = sb.tile([P, P], F32, name="ident")
+
+        nc.vector.memset(key_bytes[:].bitcast(I32), 0)
+        nc.sync.dma_start(offsets[:], offs)
+        nc.sync.dma_start(key_words[:].bitcast(I32), keys_words[0].bitcast(I32))
+        nc.sync.dma_start(q_raw[:], query.rearrange("(p j) q -> p j q", j=PACK))
+        for r in range(4):
+            nc.sync.dma_start(key_bytes[r:P:32, :].bitcast(I32), keys_scales[0, r:16:4, :].bitcast(I32))
+        nc.sync.dma_start(v_pool[0][:], vals[0:P, :])
+        nc.sync.dma_start(m0_sb[:], m0)
+        nc.sync.dma_start(v_pool[1][:], vals[P : 2 * P, :])
+        nc.sync.dma_start(size_sb[:], size.rearrange("o (p t) -> p (o t)", t=PACK))
+        nc.sync.dma_start(z0_sb[:], z0)
+        for b in range(2, BLOCKS):
+            nc.sync.dma_start(v_pool[b][:], vals[b * P : (b + 1) * P, :])
+        nc.sync.dma_start(o0_sb[:], o0)
+        make_identity(nc, ident[:])
+
+        neg_m0 = sb.tile([P, 1], F32, name="neg_m0")
+        nc.gpsimd.tensor_scalar(neg_m0[:], m0_sb[:], -1.0, 0.0, ALU.mult, ALU.add)
+
+        q_bf = sb.tile([P, Q, PACK], BF16, name="q_bf", align_bytes=64)
+        nc.scalar.copy(q_bf[:], q_raw[:].rearrange("p j q -> p q j"))
+        q_codes = sb.tile([P, Q], U32, name="q_codes", align_bytes=64)
+        q_scales = sb.tile([P, Q], U8, name="q_scales", align_bytes=64)
+
+        k_words = sb.tile([P, I], U16, name="k_words", align_bytes=64)
+        k_bytes = sb.tile([P, I], U8, name="k_bytes", align_bytes=64)
+        nc.vector.tensor_copy(k_words[:], key_words[:].indirect(offsets[:]))
+        nc.vector.tensor_copy(k_bytes[:], key_bytes[:].indirect(offsets[:]))
+        nc.vector.quantize_mx(q_codes[:].bitcast(FP8X4), q_scales[:], q_bf[:].rearrange("p q j -> p (q j)"))
+
+        scores = ps.tile([P, I], F32, name="scores")
+        nc.tensor.matmul_mx(
+            out=scores[:], lhsT=q_codes[:].bitcast(FP8X4), lhsT_scale=q_scales[:],
+            rhs=k_words[:].bitcast(FP4X4), rhs_scale=k_bytes[:], start=True, stop=True,
+        )
+
+        v_codes = [sb.tile([P, P], U32, name="v_codes%d" % b, align_bytes=64) for b in range(BLOCKS)]
+        v_scales = [sb.tile([P, P], U8, name="v_scales%d" % b, align_bytes=64) for b in range(BLOCKS)]
+        v_grouped = [sb.tile([P, P, PACK], BF16, name="v_grouped%d" % b, align_bytes=64) for b in range(BLOCKS)]
+
+        def gather_and_turn(b):
+            picked = sb.tile([P, I], BF16, name="picked%d" % b, align_bytes=64)
+            nc.vector.tensor_copy(picked[:], v_pool[b][:].indirect(offsets[:]))
+            words = picked[:].bitcast(F32)
+            turned = ps.tile([P, 2, P], F32, name="turned%d" % b)
+            for u in range(2):
+                nc.tensor.transpose(turned[:, u, :], words[:, u : I // 2 : 2], ident[:])
+            nc.scalar.copy(v_grouped[b][:].bitcast(F32), turned[:].rearrange("p u e -> p e u"))
+
+        def quantize_values(b):
+            nc.vector.quantize_mx(
+                v_codes[b][:].bitcast(FP8X4), v_scales[b][:], v_grouped[b][:].rearrange("p e t -> p (e t)")
+            )
+
+        neg_scores = sb.tile([P, PACK, P], F32, name="neg_scores")
+        neg_m1 = sb.tile([P, 1], F32, name="neg_m1")
+        nc.vector.tensor_scalar(
+            neg_scores[:], scores[:].rearrange("q (p t) -> q t p", t=PACK), -1.0, neg_m0[:],
+            ALU.mult, ALU.min, accum_out=neg_m1[:],
+        )
+        probs = sb.tile([P, PACK, P], F32, name="probs")
+        p_sum = sb.tile([P, 1], F32, name="p_sum")
+        nc.scalar.activation(probs[:], neg_scores[:], ACT.Exp, bias=neg_m1[:], scale=-1.0, accum_out=p_sum[:])
+        gather_and_turn(0)
+        probs_t = ps.tile([P, PACK, Q], F32, name="probs_t")
+        for t in range(PACK):
+            nc.tensor.transpose(probs_t[:, t, :], probs[:, t, :], ident[:])
+
+        e0 = sb.tile([P, 1], F32, name="e0")
+        r0 = sb.tile([P, 1], F32, name="r0")
+        z = sb.tile([P, 1], F32, name="z")
+        rz = sb.tile([P, 1], F32, name="rz")
+        c0 = sb.tile([P, 1], F32, name="c0")
+        nc.scalar.activation(e0[:], m0_sb[:], ACT.Exp, bias=neg_m1[:], scale=1.0)
+        nc.scalar.activation(r0[:], e0[:], ACT.Copy, scale=z0_sb[:])
+        nc.scalar.activation(z[:], p_sum[:], ACT.Identity, bias=r0[:], scale=1.0)
+
+        w_bf = sb.tile([P, Q, PACK], BF16, name="w_bf", align_bytes=64)
+        nc.vector.tensor_tensor(
+            w_bf[:], probs_t[:].rearrange("p t q -> p q t"),
+            size_sb[:].unsqueeze(1).to_broadcast([P, Q, PACK]), ALU.mult,
+        )
+        quantize_values(0)
+        nc.vector.reciprocal(rz[:], z[:])
+        w_codes = sb.tile([P, Q], U32, name="w_codes", align_bytes=64)
+        w_scales = sb.tile([P, Q], U8, name="w_scales", align_bytes=64)
+        nc.vector.quantize_mx(w_codes[:].bitcast(FP8X4), w_scales[:], w_bf[:].rearrange("p q t -> p (q t)"))
+        nc.scalar.activation(c0[:], r0[:], ACT.Copy, scale=rz[:])
+
+        early = (BLOCKS - 1) * P
+        acc_early = ps.tile([P, early], F32, name="acc_early")
+        acc_last = ps.tile([P, P], F32, name="acc_last")
+
+        def product(b, acc):
+            nc.tensor.matmul_mx(
+                out=acc, lhsT=w_codes[:].bitcast(FP8X4), lhsT_scale=w_scales[:],
+                rhs=v_codes[b][:].bitcast(FP8X4), rhs_scale=v_scales[b][:], start=True, stop=True,
+            )
+
+        product(0, acc_early[:, 0:P])
+        for b in range(1, BLOCKS - 1):
+            gather_and_turn(b)
+            quantize_values(b)
+            product(b, acc_early[:, b * P : (b + 1) * P])
+
+        o0_scaled = sb.tile([P, E], F32, name="o0_scaled")
+        nc.scalar.activation(o0_scaled[:], o0_sb[:], ACT.Copy, scale=c0[:])
+        gather_and_turn(BLOCKS - 1)
+
+        res_early = sb.tile([P, early], F32, name="res_early")
+        nc.vector.scalar_tensor_tensor(res_early[:], acc_early[:], rz[:], o0_scaled[:, 0:early], ALU.mult, ALU.add)
+        nc.sync.dma_start(out[:, 0:early], res_early[:])
+
+        quantize_values(BLOCKS - 1)
+        product(BLOCKS - 1, acc_last[:])
+        res_last = sb.tile([P, P], F32, name="res_last")
+        nc.vector.scalar_tensor_tensor(res_last[:], acc_last[:], rz[:], o0_scaled[:, early:E], ALU.mult, ALU.add)
+        nc.sync.dma_start(out[:, early:E], res_last[:])

@@ -19,7 +19,10 @@ ACT = mybir.ActivationFunctionType
 
 P = 128
 PACK = 4
+QUADRANT = 32
+SCALE_ROWS = D // 32
 BLOCKS = E // P
+ALIGN = 64
 
 
 def tile_attend_resumedread_kernel(tc, query, keys_words, keys_scales, m0, z0, o0, size, vals, offs, out):
@@ -28,23 +31,28 @@ def tile_attend_resumedread_kernel(tc, query, keys_words, keys_scales, m0, z0, o
         sb = ctx.enter_context(tc.tile_pool(name="sb", bufs=1))
         ps = ctx.enter_context(tc.psum_pool(name="ps", bufs=1))
 
+        def aligned(shape, dtype, name, tag=None):
+            return sb.tile(shape, dtype, name=name, tag=tag or name, align_bytes=ALIGN)
+
         offsets = sb.tile([P, I // 16], U16, name="offsets")
-        key_words = sb.tile([P, T], U16, name="key_words", align_bytes=64)
-        key_bytes = sb.tile([P, T], U8, name="key_bytes", align_bytes=64)
+        pool_words = aligned([P, T], U16, "pool_words")
+        pool_scales = aligned([P, T], U8, "pool_scales")
         q_raw = sb.tile([P, PACK, Q], F32, name="q_raw")
-        v_pool = [sb.tile([P, T], F32, name="v_pool%d" % b) for b in range(BLOCKS)]
+        v_pool = [aligned([P, T], F32, "v_pool%d" % b) for b in range(BLOCKS)]
         m0_sb = sb.tile([P, 1], F32, name="m0_sb")
         z0_sb = sb.tile([P, 1], F32, name="z0_sb")
         size_sb = sb.tile([P, PACK], F32, name="size_sb")
         o0_sb = sb.tile([P, E], F32, name="o0_sb")
         ident = sb.tile([P, P], F32, name="ident")
 
-        nc.vector.memset(key_bytes[:].bitcast(I32), 0)
+        nc.vector.memset(pool_scales[:].bitcast(I32), 0)
+        nc.sync.dma_start(pool_words[:].bitcast(I32), keys_words[0].bitcast(I32))
         nc.sync.dma_start(offsets[:], offs)
-        nc.sync.dma_start(key_words[:].bitcast(I32), keys_words[0].bitcast(I32))
-        nc.sync.dma_start(q_raw[:], query.rearrange("(p j) q -> p j q", j=PACK))
-        for r in range(4):
-            nc.sync.dma_start(key_bytes[r:P:32, :].bitcast(I32), keys_scales[0, r:16:4, :].bitcast(I32))
+        for r in range(PACK):
+            nc.sync.dma_start(
+                pool_scales[r:P:QUADRANT, :].bitcast(I32), keys_scales[0, r:SCALE_ROWS:PACK, :].bitcast(I32)
+            )
+        nc.sync.dma_start(q_raw[:], query.rearrange("(p t) q -> p t q", t=PACK))
         nc.sync.dma_start(v_pool[0][:], vals[0:P, :])
         nc.sync.dma_start(m0_sb[:], m0)
         nc.sync.dma_start(v_pool[1][:], vals[P : 2 * P, :])
@@ -58,102 +66,122 @@ def tile_attend_resumedread_kernel(tc, query, keys_words, keys_scales, m0, z0, o
         neg_m0 = sb.tile([P, 1], F32, name="neg_m0")
         nc.gpsimd.tensor_scalar(neg_m0[:], m0_sb[:], -1.0, 0.0, ALU.mult, ALU.add)
 
-        q_bf = sb.tile([P, Q, PACK], BF16, name="q_bf", align_bytes=64)
-        nc.scalar.copy(q_bf[:], q_raw[:].rearrange("p j q -> p q j"))
-        q_codes = sb.tile([P, Q], U32, name="q_codes", align_bytes=64)
-        q_scales = sb.tile([P, Q], U8, name="q_scales", align_bytes=64)
-
-        k_words = sb.tile([P, I], U16, name="k_words", align_bytes=64)
-        k_bytes = sb.tile([P, I], U8, name="k_bytes", align_bytes=64)
-        nc.vector.tensor_copy(k_words[:], key_words[:].indirect(offsets[:]))
-        nc.vector.tensor_copy(k_bytes[:], key_bytes[:].indirect(offsets[:]))
-        nc.vector.quantize_mx(q_codes[:].bitcast(FP8X4), q_scales[:], q_bf[:].rearrange("p q j -> p (q j)"))
-
-        scores = ps.tile([P, I], F32, name="scores")
+        q_bf = aligned([P, Q, PACK], BF16, "q_bf")
+        nc.scalar.copy(q_bf[:], q_raw[:].rearrange("p t q -> p q t"))
+        q_codes = aligned([P, Q], U32, "q_codes")
+        q_scales = aligned([P, Q], U8, "q_scales")
+        k_words = aligned([P, I], U16, "k_words")
+        k_scales = aligned([P, I], U8, "k_scales")
+        nc.vector.tensor_copy(k_words[:], pool_words[:].indirect(offsets[:]))
+        nc.vector.tensor_copy(k_scales[:], pool_scales[:].indirect(offsets[:]))
+        nc.vector.quantize_mx(q_codes[:].bitcast(FP8X4), q_scales[:], q_bf[:].rearrange("p q t -> p (q t)"))
+        scores = ps.tile([P, I], F32, name="scores", tag="scores")
         nc.tensor.matmul_mx(
-            out=scores[:], lhsT=q_codes[:].bitcast(FP8X4), lhsT_scale=q_scales[:],
-            rhs=k_words[:].bitcast(FP4X4), rhs_scale=k_bytes[:], start=True, stop=True,
+            out=scores[:],
+            lhsT=q_codes[:].bitcast(FP8X4),
+            lhsT_scale=q_scales[:],
+            rhs=k_words[:].bitcast(FP4X4),
+            rhs_scale=k_scales[:],
+            start=True,
+            stop=True,
         )
 
-        v_codes = [sb.tile([P, P], U32, name="v_codes%d" % b, align_bytes=64) for b in range(BLOCKS)]
-        v_scales = [sb.tile([P, P], U8, name="v_scales%d" % b, align_bytes=64) for b in range(BLOCKS)]
-        v_grouped = [sb.tile([P, P, PACK], BF16, name="v_grouped%d" % b, align_bytes=64) for b in range(BLOCKS)]
+        neg_scores = aligned([P, I], F32, "neg_scores")
+        neg_m1 = sb.tile([P, 1], F32, name="neg_m1")
+        nc.vector.tensor_scalar(neg_scores[:], scores[:], -1.0, neg_m0[:], ALU.mult, ALU.min, accum_out=neg_m1[:])
+        probs = sb.tile([P, PACK, P], F32, name="probs")
+        p_sum = sb.tile([P, 1], F32, name="p_sum")
+        nc.scalar.activation(
+            probs[:].rearrange("q t p -> q p t"),
+            neg_scores[:].rearrange("q (p t) -> q p t", t=PACK),
+            ACT.Exp,
+            bias=neg_m1[:],
+            scale=-1.0,
+            accum_out=p_sum[:],
+        )
+
+        w_and_v0 = aligned([P, 2 * I], BF16, "w_and_v0", tag="neg_scores")
+        v_bf = [w_and_v0[:, I : 2 * I]] + [aligned([P, I], BF16, "v_bf%d" % b)[:] for b in range(1, BLOCKS)]
 
         def gather_and_turn(b):
-            picked = sb.tile([P, I], BF16, name="picked%d" % b, align_bytes=64)
+            picked = aligned([P, I], BF16, "picked%d" % b)
             nc.vector.tensor_copy(picked[:], v_pool[b][:].indirect(offsets[:]))
             words = picked[:].bitcast(F32)
             turned = ps.tile([P, 2, P], F32, name="turned%d" % b)
             for u in range(2):
                 nc.tensor.transpose(turned[:, u, :], words[:, u : I // 2 : 2], ident[:])
-            nc.scalar.copy(v_grouped[b][:].bitcast(F32), turned[:].rearrange("p u e -> p e u"))
-
-        def quantize_values(b):
-            nc.vector.quantize_mx(
-                v_codes[b][:].bitcast(FP8X4), v_scales[b][:], v_grouped[b][:].rearrange("p e t -> p (e t)")
+            nc.scalar.copy(
+                v_bf[b].bitcast(F32).rearrange("p (e u) -> p e u", u=2), turned[:].rearrange("p u e -> p e u")
             )
 
-        neg_scores = sb.tile([P, PACK, P], F32, name="neg_scores")
-        neg_m1 = sb.tile([P, 1], F32, name="neg_m1")
-        nc.vector.tensor_scalar(
-            neg_scores[:], scores[:].rearrange("q (p t) -> q t p", t=PACK), -1.0, neg_m0[:],
-            ALU.mult, ALU.min, accum_out=neg_m1[:],
-        )
-        probs = sb.tile([P, PACK, P], F32, name="probs")
-        p_sum = sb.tile([P, 1], F32, name="p_sum")
-        nc.scalar.activation(probs[:], neg_scores[:], ACT.Exp, bias=neg_m1[:], scale=-1.0, accum_out=p_sum[:])
         gather_and_turn(0)
         probs_t = ps.tile([P, PACK, Q], F32, name="probs_t")
         for t in range(PACK):
             nc.tensor.transpose(probs_t[:, t, :], probs[:, t, :], ident[:])
 
-        e0 = sb.tile([P, 1], F32, name="e0")
+        decay = sb.tile([P, 1], F32, name="decay")
         r0 = sb.tile([P, 1], F32, name="r0")
         z = sb.tile([P, 1], F32, name="z")
-        rz = sb.tile([P, 1], F32, name="rz")
-        c0 = sb.tile([P, 1], F32, name="c0")
-        nc.scalar.activation(e0[:], m0_sb[:], ACT.Exp, bias=neg_m1[:], scale=1.0)
-        nc.scalar.activation(r0[:], e0[:], ACT.Copy, scale=z0_sb[:])
-        nc.scalar.activation(z[:], p_sum[:], ACT.Identity, bias=r0[:], scale=1.0)
+        kept_share = sb.tile([P, 1], F32, name="kept_share")
+        nc.scalar.activation(decay[:], m0_sb[:], ACT.Exp, bias=neg_m1[:], scale=1.0)
+        nc.gpsimd.tensor_scalar(r0[:], decay[:], z0_sb[:], 0.0, ALU.mult, ALU.add)
+        nc.gpsimd.tensor_scalar(z[:], decay[:], z0_sb[:], p_sum[:], ALU.mult, ALU.add)
 
-        w_bf = sb.tile([P, Q, PACK], BF16, name="w_bf", align_bytes=64)
+        gather_and_turn(1)
+        inv_z = aligned([P, 1], F32, "inv_z", tag="v_pool1")
+        nc.vector.reciprocal(inv_z[:], z[:])
+        nc.gpsimd.tensor_scalar(kept_share[:], r0[:], inv_z[:], 0.0, ALU.mult, ALU.add)
+
         nc.vector.tensor_tensor(
-            w_bf[:], probs_t[:].rearrange("p t q -> p q t"),
-            size_sb[:].unsqueeze(1).to_broadcast([P, Q, PACK]), ALU.mult,
+            w_and_v0[:, 0:I].rearrange("p (q t) -> p q t", t=PACK),
+            probs_t[:].rearrange("p t q -> p q t"),
+            size_sb[:].unsqueeze(1).to_broadcast([P, Q, PACK]),
+            ALU.mult,
         )
-        quantize_values(0)
-        nc.vector.reciprocal(rz[:], z[:])
-        w_codes = sb.tile([P, Q], U32, name="w_codes", align_bytes=64)
-        w_scales = sb.tile([P, Q], U8, name="w_scales", align_bytes=64)
-        nc.vector.quantize_mx(w_codes[:].bitcast(FP8X4), w_scales[:], w_bf[:].rearrange("p q t -> p (q t)"))
-        nc.scalar.activation(c0[:], r0[:], ACT.Copy, scale=rz[:])
 
-        early = (BLOCKS - 1) * P
-        acc_early = ps.tile([P, early], F32, name="acc_early")
-        acc_last = ps.tile([P, P], F32, name="acc_last")
+        gather_and_turn(2)
+        codes_w01 = aligned([P, 3 * P], U32, "codes_w01", tag="v_pool2")
+        scales_w01 = aligned([P, 3 * P], U8, "scales_w01")
+        nc.vector.quantize_mx(codes_w01[:, 0 : 2 * P].bitcast(FP8X4), scales_w01[:, 0 : 2 * P], w_and_v0[:])
+        nc.vector.quantize_mx(codes_w01[:, 2 * P : 3 * P].bitcast(FP8X4), scales_w01[:, 2 * P : 3 * P], v_bf[1])
 
-        def product(b, acc):
+        def product(acc, codes, scales):
             nc.tensor.matmul_mx(
-                out=acc, lhsT=w_codes[:].bitcast(FP8X4), lhsT_scale=w_scales[:],
-                rhs=v_codes[b][:].bitcast(FP8X4), rhs_scale=v_scales[b][:], start=True, stop=True,
+                out=acc,
+                lhsT=codes_w01[:, 0:P].bitcast(FP8X4),
+                lhsT_scale=scales_w01[:, 0:P],
+                rhs=codes.bitcast(FP8X4),
+                rhs_scale=scales,
+                start=True,
+                stop=True,
             )
 
-        product(0, acc_early[:, 0:P])
-        for b in range(1, BLOCKS - 1):
-            gather_and_turn(b)
-            quantize_values(b)
-            product(b, acc_early[:, b * P : (b + 1) * P])
+        def quantize_and_multiply(b, codes_tag, acc):
+            codes = aligned([P, P], U32, "codes%d" % b, tag=codes_tag)
+            scales = aligned([P, P], U8, "scales%d" % b)
+            nc.vector.quantize_mx(codes[:].bitcast(FP8X4), scales[:], v_bf[b])
+            product(acc, codes[:], scales[:])
 
-        o0_scaled = sb.tile([P, E], F32, name="o0_scaled")
-        nc.scalar.activation(o0_scaled[:], o0_sb[:], ACT.Copy, scale=c0[:])
-        gather_and_turn(BLOCKS - 1)
+        def finish(result, acc, kept, first_column):
+            nc.vector.scalar_tensor_tensor(result, acc, inv_z[:], kept, ALU.mult, ALU.add)
+            nc.sync.dma_start(out[:, first_column : first_column + result.shape[1]], result)
 
-        res_early = sb.tile([P, early], F32, name="res_early")
-        nc.vector.scalar_tensor_tensor(res_early[:], acc_early[:], rz[:], o0_scaled[:, 0:early], ALU.mult, ALU.add)
-        nc.sync.dma_start(out[:, 0:early], res_early[:])
+        acc01 = ps.tile([P, 2 * P], F32, name="acc01")
+        product(acc01[:], codes_w01[:, P : 3 * P], scales_w01[:, P : 3 * P])
 
-        quantize_values(BLOCKS - 1)
-        product(BLOCKS - 1, acc_last[:])
-        res_last = sb.tile([P, P], F32, name="res_last")
-        nc.vector.scalar_tensor_tensor(res_last[:], acc_last[:], rz[:], o0_scaled[:, early:E], ALU.mult, ALU.add)
-        nc.sync.dma_start(out[:, early:E], res_last[:])
+        gather_and_turn(3)
+        kept01 = aligned([P, 2 * P], F32, "kept01")
+        kept23 = sb.tile([P, 2 * P], F32, name="kept23")
+        nc.scalar.activation(kept01[:], o0_sb[:, 0 : 2 * P], ACT.Copy, scale=kept_share[:])
+        nc.scalar.activation(kept23[:], o0_sb[:, 2 * P : E], ACT.Copy, scale=kept_share[:])
+        acc2 = ps.tile([P, P], F32, name="acc2", tag="scores")
+        quantize_and_multiply(2, "v_pool3", acc2[:])
+        result01 = aligned([P, 2 * P], F32, "result01", tag="v_bf2")
+        finish(result01[:], acc01[:], kept01[:], 0)
+
+        acc3 = ps.tile([P, P], F32, name="acc3")
+        quantize_and_multiply(3, "kept01", acc3[:])
+        result2 = sb.tile([P, P], F32, name="result2")
+        finish(result2[:], acc2[:], kept23[:, 0:P], 2 * P)
+        result3 = sb.tile([P, P], F32, name="result3")
+        finish(result3[:], acc3[:], kept23[:, P : 2 * P], 3 * P)

@@ -19,9 +19,13 @@ ACT = mybir.ActivationFunctionType
 
 P = 128
 PACK = 4
+MX_BLOCK = 32
+SCALE_ROWS = D // MX_BLOCK
 QUADRANT = 32
-SCALE_ROWS = D // 32
-BLOCKS = E // P
+QUADRANT_ROWS = 4
+LIST_GROUP = 16
+PAIR = 2
+PARTS = E // P
 ALIGN = 64
 
 
@@ -34,11 +38,11 @@ def tile_attend_resumedread_kernel(tc, query, keys_words, keys_scales, m0, z0, o
         def aligned(shape, dtype, name, tag=None):
             return sb.tile(shape, dtype, name=name, tag=tag or name, align_bytes=ALIGN)
 
-        offsets = sb.tile([P, I // 16], U16, name="offsets")
+        offsets = sb.tile([P, I // LIST_GROUP], U16, name="offsets")
         pool_words = aligned([P, T], U16, "pool_words")
         pool_scales = aligned([P, T], U8, "pool_scales")
         q_raw = sb.tile([P, PACK, Q], F32, name="q_raw")
-        v_pool = [aligned([P, T], F32, "v_pool%d" % b) for b in range(BLOCKS)]
+        v_pool = [aligned([P, T], F32, "v_pool%d" % b) for b in range(PARTS)]
         m0_sb = sb.tile([P, 1], F32, name="m0_sb")
         z0_sb = sb.tile([P, 1], F32, name="z0_sb")
         size_sb = sb.tile([P, PACK], F32, name="size_sb")
@@ -48,9 +52,9 @@ def tile_attend_resumedread_kernel(tc, query, keys_words, keys_scales, m0, z0, o
         nc.vector.memset(pool_scales[:].bitcast(I32), 0)
         nc.sync.dma_start(pool_words[:].bitcast(I32), keys_words[0].bitcast(I32))
         nc.sync.dma_start(offsets[:], offs)
-        for r in range(PACK):
+        for r in range(QUADRANT_ROWS):
             nc.sync.dma_start(
-                pool_scales[r:P:QUADRANT, :].bitcast(I32), keys_scales[0, r:SCALE_ROWS:PACK, :].bitcast(I32)
+                pool_scales[r:P:QUADRANT, :].bitcast(I32), keys_scales[0, r:SCALE_ROWS:QUADRANT_ROWS, :].bitcast(I32)
             )
         nc.sync.dma_start(q_raw[:], query.rearrange("(p t) q -> p t q", t=PACK))
         nc.sync.dma_start(v_pool[0][:], vals[0:P, :])
@@ -58,7 +62,7 @@ def tile_attend_resumedread_kernel(tc, query, keys_words, keys_scales, m0, z0, o
         nc.sync.dma_start(v_pool[1][:], vals[P : 2 * P, :])
         nc.sync.dma_start(size_sb[:], size.rearrange("o (p t) -> p (o t)", t=PACK))
         nc.sync.dma_start(z0_sb[:], z0)
-        for b in range(2, BLOCKS):
+        for b in range(2, PARTS):
             nc.sync.dma_start(v_pool[b][:], vals[b * P : (b + 1) * P, :])
         nc.sync.dma_start(o0_sb[:], o0)
         make_identity(nc, ident[:])
@@ -101,17 +105,17 @@ def tile_attend_resumedread_kernel(tc, query, keys_words, keys_scales, m0, z0, o
         )
 
         w_and_v0 = aligned([P, 2 * I], BF16, "w_and_v0", tag="neg_scores")
-        v_bf = [w_and_v0[:, I : 2 * I]] + [aligned([P, I], BF16, "v_bf%d" % b)[:] for b in range(1, BLOCKS)]
+        v_bf = [w_and_v0[:, I : 2 * I]] + [aligned([P, I], BF16, "v_bf%d" % b)[:] for b in range(1, PARTS)]
 
         def gather_and_turn(b):
-            picked = aligned([P, I], BF16, "picked%d" % b)
-            nc.vector.tensor_copy(picked[:], v_pool[b][:].indirect(offsets[:]))
-            words = picked[:].bitcast(F32)
-            turned = ps.tile([P, 2, P], F32, name="turned%d" % b)
-            for u in range(2):
-                nc.tensor.transpose(turned[:, u, :], words[:, u : I // 2 : 2], ident[:])
+            picked = aligned([P, PAIR, P, PAIR], BF16, "picked%d" % b)
+            nc.vector.tensor_copy(picked[:].rearrange("e u w s -> e w u s"), v_pool[b][:].indirect(offsets[:]))
+            words = picked[:].rearrange("e u w s -> e (u w s)").bitcast(F32)
+            turned = ps.tile([P, PAIR, P], F32, name="turned%d" % b)
+            for u in range(PAIR):
+                nc.tensor.transpose(turned[:, u, :], words[:, u * P : (u + 1) * P], ident[:])
             nc.scalar.copy(
-                v_bf[b].bitcast(F32).rearrange("p (e u) -> p e u", u=2), turned[:].rearrange("p u e -> p e u")
+                v_bf[b].bitcast(F32).rearrange("p (e u) -> p e u", u=PAIR), turned[:].rearrange("p u e -> p e u")
             )
 
         gather_and_turn(0)

from contextlib import ExitStack

import concourse.mybir as mybir
from concourse.masks import make_identity

D, T, I, Q, E = 512, 2048, 512, 128, 512
FLOPS = 2 * Q * I * D + 2 * Q * I * E

F32 = mybir.dt.float32
BF16 = mybir.dt.bfloat16
I32 = mybir.dt.int32
U32 = mybir.dt.uint32
U16 = mybir.dt.uint16
U8 = mybir.dt.uint8
FP8X4 = mybir.dt.float8_e4m3fn_x4
FP4X4 = mybir.dt.float4_e2m1fn_x4
ALU = mybir.AluOpType
ACT = mybir.ActivationFunctionType

P = 128
PACK = 4
MX_BLOCK = 32
SCALE_ROWS = D // MX_BLOCK
QUADRANT = 32
QUADRANT_ROWS = 4
LIST_GROUP = 16
PAIR = 2
PARTS = E // P
ALIGN = 64


def tile_attend_resumedread_kernel(tc, query, keys_words, keys_scales, m0, z0, o0, size, vals, offs, out):
    nc = tc.nc
    with ExitStack() as ctx:
        sb = ctx.enter_context(tc.tile_pool(name="sb", bufs=1))
        ps = ctx.enter_context(tc.psum_pool(name="ps", bufs=1))

        def aligned(shape, dtype, name, tag=None):
            return sb.tile(shape, dtype, name=name, tag=tag or name, align_bytes=ALIGN)

        offsets = sb.tile([P, I // LIST_GROUP], U16, name="offsets")
        pool_words = aligned([P, T], U16, "pool_words")
        pool_scales = aligned([P, T], U8, "pool_scales")
        q_raw = sb.tile([P, PACK, Q], F32, name="q_raw")
        v_pool = [aligned([P, T], F32, "v_pool%d" % b) for b in range(PARTS)]
        m0_sb = sb.tile([P, 1], F32, name="m0_sb")
        z0_sb = sb.tile([P, 1], F32, name="z0_sb")
        size_sb = sb.tile([P, PACK], F32, name="size_sb")
        o0_sb = sb.tile([P, E], F32, name="o0_sb")
        ident = sb.tile([P, P], F32, name="ident")

        nc.vector.memset(pool_scales[:].bitcast(I32), 0)
        nc.sync.dma_start(pool_words[:].bitcast(I32), keys_words[0].bitcast(I32))
        nc.sync.dma_start(offsets[:], offs)
        for r in range(QUADRANT_ROWS):
            nc.sync.dma_start(
                pool_scales[r:P:QUADRANT, :].bitcast(I32), keys_scales[0, r:SCALE_ROWS:QUADRANT_ROWS, :].bitcast(I32)
            )
        nc.sync.dma_start(q_raw[:], query.rearrange("(p t) q -> p t q", t=PACK))
        nc.sync.dma_start(v_pool[0][:], vals[0:P, :])
        nc.sync.dma_start(m0_sb[:], m0)
        nc.sync.dma_start(v_pool[1][:], vals[P : 2 * P, :])
        nc.sync.dma_start(size_sb[:], size.rearrange("o (p t) -> p (o t)", t=PACK))
        nc.sync.dma_start(z0_sb[:], z0)
        for b in range(2, PARTS):
            nc.sync.dma_start(v_pool[b][:], vals[b * P : (b + 1) * P, :])
        nc.sync.dma_start(o0_sb[:], o0)
        make_identity(nc, ident[:])

        neg_m0 = sb.tile([P, 1], F32, name="neg_m0")
        nc.gpsimd.tensor_scalar(neg_m0[:], m0_sb[:], -1.0, 0.0, ALU.mult, ALU.add)

        q_bf = aligned([P, Q, PACK], BF16, "q_bf")
        nc.scalar.copy(q_bf[:], q_raw[:].rearrange("p t q -> p q t"))
        q_codes = aligned([P, Q], U32, "q_codes")
        q_scales = aligned([P, Q], U8, "q_scales")
        k_words = aligned([P, I], U16, "k_words")
        k_scales = aligned([P, I], U8, "k_scales")
        nc.vector.tensor_copy(k_words[:], pool_words[:].indirect(offsets[:]))
        nc.vector.tensor_copy(k_scales[:], pool_scales[:].indirect(offsets[:]))
        nc.vector.quantize_mx(q_codes[:].bitcast(FP8X4), q_scales[:], q_bf[:].rearrange("p q t -> p (q t)"))
        scores = ps.tile([P, I], F32, name="scores", tag="scores")
        nc.tensor.matmul_mx(
            out=scores[:],
            lhsT=q_codes[:].bitcast(FP8X4),
            lhsT_scale=q_scales[:],
            rhs=k_words[:].bitcast(FP4X4),
            rhs_scale=k_scales[:],
            start=True,
            stop=True,
        )

        neg_scores = aligned([P, I], F32, "neg_scores")
        neg_m1 = sb.tile([P, 1], F32, name="neg_m1")
        nc.vector.tensor_scalar(neg_scores[:], scores[:], -1.0, neg_m0[:], ALU.mult, ALU.min, accum_out=neg_m1[:])
        probs = sb.tile([P, PACK, P], F32, name="probs")
        p_sum = sb.tile([P, 1], F32, name="p_sum")
        nc.scalar.activation(
            probs[:].rearrange("q t p -> q p t"),
            neg_scores[:].rearrange("q (p t) -> q p t", t=PACK),
            ACT.Exp,
            bias=neg_m1[:],
            scale=-1.0,
            accum_out=p_sum[:],
        )

        w_and_v0 = aligned([P, 2 * I], BF16, "w_and_v0", tag="neg_scores")
        v_bf = [w_and_v0[:, I : 2 * I]] + [aligned([P, I], BF16, "v_bf%d" % b)[:] for b in range(1, PARTS)]

        def gather_and_turn(b):
            picked = aligned([P, PAIR, P, PAIR], BF16, "picked%d" % b)
            nc.vector.tensor_copy(picked[:].rearrange("e u w s -> e w u s"), v_pool[b][:].indirect(offsets[:]))
            words = picked[:].rearrange("e u w s -> e (u w s)").bitcast(F32)
            turned = ps.tile([P, PAIR, P], F32, name="turned%d" % b)
            for u in range(PAIR):
                nc.tensor.transpose(turned[:, u, :], words[:, u * P : (u + 1) * P], ident[:])
            nc.scalar.copy(
                v_bf[b].bitcast(F32).rearrange("p (e u) -> p e u", u=PAIR), turned[:].rearrange("p u e -> p e u")
            )

        gather_and_turn(0)
        probs_t = ps.tile([P, PACK, Q], F32, name="probs_t")
        for t in range(PACK):
            nc.tensor.transpose(probs_t[:, t, :], probs[:, t, :], ident[:])

        decay = sb.tile([P, 1], F32, name="decay")
        r0 = sb.tile([P, 1], F32, name="r0")
        z = sb.tile([P, 1], F32, name="z")
        kept_share = sb.tile([P, 1], F32, name="kept_share")
        nc.scalar.activation(decay[:], m0_sb[:], ACT.Exp, bias=neg_m1[:], scale=1.0)
        nc.gpsimd.tensor_scalar(r0[:], decay[:], z0_sb[:], 0.0, ALU.mult, ALU.add)
        nc.gpsimd.tensor_scalar(z[:], decay[:], z0_sb[:], p_sum[:], ALU.mult, ALU.add)

        gather_and_turn(1)
        inv_z = aligned([P, 1], F32, "inv_z", tag="v_pool1")
        nc.vector.reciprocal(inv_z[:], z[:])
        nc.gpsimd.tensor_scalar(kept_share[:], r0[:], inv_z[:], 0.0, ALU.mult, ALU.add)

        nc.vector.tensor_tensor(
            w_and_v0[:, 0:I].rearrange("p (q t) -> p q t", t=PACK),
            probs_t[:].rearrange("p t q -> p q t"),
            size_sb[:].unsqueeze(1).to_broadcast([P, Q, PACK]),
            ALU.mult,
        )

        gather_and_turn(2)
        codes_w01 = aligned([P, 3 * P], U32, "codes_w01", tag="v_pool2")
        scales_w01 = aligned([P, 3 * P], U8, "scales_w01")
        nc.vector.quantize_mx(codes_w01[:, 0 : 2 * P].bitcast(FP8X4), scales_w01[:, 0 : 2 * P], w_and_v0[:])
        nc.vector.quantize_mx(codes_w01[:, 2 * P : 3 * P].bitcast(FP8X4), scales_w01[:, 2 * P : 3 * P], v_bf[1])

        def product(acc, codes, scales):
            nc.tensor.matmul_mx(
                out=acc,
                lhsT=codes_w01[:, 0:P].bitcast(FP8X4),
                lhsT_scale=scales_w01[:, 0:P],
                rhs=codes.bitcast(FP8X4),
                rhs_scale=scales,
                start=True,
                stop=True,
            )

        def quantize_and_multiply(b, codes_tag, acc):
            codes = aligned([P, P], U32, "codes%d" % b, tag=codes_tag)
            scales = aligned([P, P], U8, "scales%d" % b)
            nc.vector.quantize_mx(codes[:].bitcast(FP8X4), scales[:], v_bf[b])
            product(acc, codes[:], scales[:])

        def finish(result, acc, kept, first_column):
            nc.vector.scalar_tensor_tensor(result, acc, inv_z[:], kept, ALU.mult, ALU.add)
            nc.sync.dma_start(out[:, first_column : first_column + result.shape[1]], result)

        acc01 = ps.tile([P, 2 * P], F32, name="acc01")
        product(acc01[:], codes_w01[:, P : 3 * P], scales_w01[:, P : 3 * P])

        gather_and_turn(3)
        kept01 = aligned([P, 2 * P], F32, "kept01")
        kept23 = sb.tile([P, 2 * P], F32, name="kept23")
        nc.scalar.activation(kept01[:], o0_sb[:, 0 : 2 * P], ACT.Copy, scale=kept_share[:])
        nc.scalar.activation(kept23[:], o0_sb[:, 2 * P : E], ACT.Copy, scale=kept_share[:])
        acc2 = ps.tile([P, P], F32, name="acc2", tag="scores")
        quantize_and_multiply(2, "v_pool3", acc2[:])
        result01 = aligned([P, 2 * P], F32, "result01", tag="v_bf2")
        finish(result01[:], acc01[:], kept01[:], 0)

        acc3 = ps.tile([P, P], F32, name="acc3")
        quantize_and_multiply(3, "kept01", acc3[:])
        result2 = sb.tile([P, P], F32, name="result2")
        finish(result2[:], acc2[:], kept23[:, 0:P], 2 * P)
        result3 = sb.tile([P, P], F32, name="result3")
        finish(result3[:], acc3[:], kept23[:, P : 2 * P], 3 * P)
